import numpy as np
import ml_dtypes


def mxq(x, axis, fmt="e4m3"):
    dtype, down = {"e4m3": (ml_dtypes.float8_e4m3fn, 7), "e5m2": (ml_dtypes.float8_e5m2, 14)}[fmt]
    v = np.moveaxis(np.asarray(x, np.float32).astype(ml_dtypes.bfloat16).astype(np.float64), axis, -1)
    blocks = v.reshape(v.shape[:-1] + (-1, 32))
    amax = np.abs(blocks).max(-1, keepdims=True)
    byte = np.maximum(np.where(amax > 0, np.frexp(amax)[1] - 1 + 127, 0) - down, 1)
    scale = np.exp2(byte - 127.0)
    codes = (blocks / scale).astype(np.float32).astype(dtype).astype(np.float64)
    return np.moveaxis((codes * scale).reshape(v.shape), -1, axis)


WIDE = False


def mx_kscale(k):
    if not WIDE:
        return np.ones(k)
    levels = np.array([10, -10, 5, -5, 0])
    if k % 512:
        return np.exp2(np.random.permutation(np.resize(levels, k // 32))).repeat(32)
    a = np.empty((k // 512, 16))
    for p in range(k // 512):
        a[p, :8] = np.random.permutation(np.resize(levels, 8))
        for g in range(8):
            far = levels[np.abs(levels - a[p, g]) >= 10]
            a[p, g + 8] = far[np.random.randint(len(far))]
    return np.exp2(a.ravel()).repeat(32)


def f64(x):
    return np.asarray(x).astype(np.float64)


def striped(idx):
    return np.tile(idx.reshape(-1, 16).T, (8, 1)).astype(np.uint16)


def unstriped(offs):
    return offs[:16].T.reshape(-1).astype(np.int64)


def pack_weight(w):
    k, n = w.shape
    w = f64(np.asarray(w, np.float32).astype(ml_dtypes.bfloat16)).reshape(k // 32, 32, n)
    amax = np.abs(w).max(1)
    byte = np.clip(np.where(amax > 0, np.frexp(amax)[1] - 1 + 127 - 7, 1), 1, 254)
    scaled = (w * np.exp2(127.0 - byte)[:, None, :]).reshape(k, n).astype(np.float32)
    words = np.ascontiguousarray(scaled.reshape(k // 512, 128, 4, n).transpose(0, 1, 3, 2)).astype(ml_dtypes.float8_e4m3fn).view(np.uint8)
    return words, np.ascontiguousarray(byte.astype(np.uint8).reshape(k // 512, 16, n))


def unpack_weight(words, scales):
    g, p, n, _ = words.shape
    vals = np.ascontiguousarray(words).view(ml_dtypes.float8_e4m3fn).astype(np.float64) * np.repeat(np.exp2(scales.astype(np.float64) - 127.0), 8, axis=1)[..., None]
    return vals.transpose(0, 1, 3, 2).reshape(g * 512, n)


def silu(v):
    return v / (1.0 + np.exp(-np.maximum(v, -700.0)))


K, T, S, N = 512, 4096, 2048, 256


def setup_inputs():
    n = np.random.standard_normal
    s = mx_kscale(K)[:, None]
    words, scales = pack_weight(n((K, N)) / np.sqrt(K) / s)
    return {
        "xT": (n((K, T)) * s).astype(np.float32),
        "w_words": words,
        "w_scales": scales,
        "b": (0.3 * n((N, 1))).astype(np.float32),
        "offs": striped(np.random.permutation(T)[:S]),
    }


def reference(xT, w_words, w_scales, b, offs):
    w = unpack_weight(w_words, w_scales)
    idx = unstriped(offs)
    xq = mxq(f64(xT)[:, idx], 0, "e4m3")
    y = w.T @ xq
    y = silu(y + f64(b))
    return y

@@ -1,0 +1,139 @@
+from contextlib import ExitStack
+
+import concourse.mybir as mybir
+
+K, T, S, N = 512, 4096, 2048, 256
+FLOPS = 2 * K * S * N
+
+F32 = mybir.dt.float32
+BF16 = mybir.dt.bfloat16
+I32 = mybir.dt.int32
+U32 = mybir.dt.uint32
+U16 = mybir.dt.uint16
+U8 = mybir.dt.uint8
+FP8X4 = mybir.dt.float8_e4m3fn_x4
+SILU = mybir.ActivationFunctionType.Silu
+
+P = 128
+PACK = 4
+HALF = T // 2
+SLICE = 512
+SLICES = S // SLICE
+LIST_COLS = SLICE // 16
+HALVES = N // P
+
+
+def tile_picked_pick_lin_silu_sub_e_kernel(tc, xT, w_words, w_scales, b, offs, out):
+    nc = tc.nc
+    with ExitStack() as ctx:
+        keep = ctx.enter_context(tc.tile_pool(name="keep", bufs=1))
+        psum = ctx.enter_context(tc.psum_pool(name="psum", bufs=8))
+
+        offsets = keep.tile([P, S // 16], U16, name="offsets")
+        w_codes = keep.tile([P, N], U32, name="w_codes", align_bytes=64)
+        w_exps = keep.tile([P, N], U8, name="w_exps", align_bytes=64)
+        bias = keep.tile([P, HALVES], F32, name="bias")
+        warm = keep.tile([P, 8], F32, name="warm")
+        warm_out = keep.tile([P, 8], F32, name="warm_out")
+        raw_low = keep.tile([P, 2, T], F32, name="raw_low")
+        raw_high = [keep.tile([P, 2, HALF], F32, name="raw_high%d" % i) for i in range(2)]
+        pairs = [keep.tile([P, 2 * T], BF16, name="pairs%d" % u, align_bytes=64) for u in range(2)]
+        picked = keep.tile([P, 2 * SLICES - 1, SLICE], U32, name="picked", align_bytes=64)
+        grouped = [keep.tile([P, PACK * SLICE], BF16, name="grouped%d" % s, align_bytes=64)[:] for s in range(SLICES - 1)]
+        grouped.append(picked[:, 5:7, :].rearrange("p u n -> p (u n)").bitcast(BF16))
+        codes = [keep.tile([P, SLICE], U32, name="codes%d" % s, align_bytes=64) for s in range(SLICES)]
+        exps = [keep.tile([P, SLICE], U8, name="exps%d" % s, align_bytes=64) for s in range(SLICES)]
+
+        planes = xT.rearrange("(p j) t -> p j t", j=PACK)
+
+        nc.vector.memset(w_exps[:].bitcast(I32), 0)
+        nc.vector.memset(warm[:], 0.0)
+        nc.scalar.activation(warm_out[:], warm[:], SILU)
+
+        def load_scales(q):
+            nc.sync.dma_start(w_exps[32 * q : 32 * q + 4, :].bitcast(I32), w_scales[0, 4 * q : 4 * q + 4, :].bitcast(I32))
+
+        nc.sync.dma_start(raw_low[:, 0, :], planes[:, 0, :])
+        nc.sync.dma_start(raw_low[:, 1, :HALF], planes[:, 1, :HALF])
+        nc.sync.dma_start(raw_low[:, 1, HALF:], planes[:, 1, HALF:])
+        nc.sync.dma_start(offsets[:], offs)
+        nc.sync.dma_start(raw_high[0][:], planes[:, 2:4, :HALF])
+        nc.sync.dma_start(raw_high[1][:, 0, :], planes[:, 2, HALF:])
+        for c0, c1 in ((0, 1024), (1024, 1536), (1536, 2048)):
+            nc.sync.dma_start(raw_high[1][:, 1, c0:c1], planes[:, 3, HALF + c0 : HALF + c1])
+        nc.sync.dma_start(w_codes[:].bitcast(I32), w_words[0].rearrange("p n t -> p (n t)").bitcast(I32))
+        with nc.allow_non_contiguous_dma(reason="one bias value to a partition"):
+            nc.sync.dma_start(bias[:], b.rearrange("(h p) o -> p (h o)", p=P))
+        for q in range(4):
+            load_scales(q)
+
+        def round_pairs(copy, u, raw, base, c0, c1):
+            copy(
+                pairs[u][:, 2 * (base + c0) : 2 * (base + c1)].rearrange("p (c e) -> p c e", e=2),
+                raw[:, :, c0:c1].rearrange("p e c -> p c e"),
+            )
+
+        def round_shared(u, raw, base, c0, c1, split):
+            round_pairs(nc.vector.tensor_copy, u, raw, base, c0, split)
+            round_pairs(nc.scalar.copy, u, raw, base, split, c1)
+
+        slot = {(0, 0): 1, (1, 0): 2, (0, 1): 3, (1, 1): 4, (0, 2): 5, (1, 2): 6, (0, 3): 0, (1, 3): 4}
+
+        def gather(u, s):
+            window = pairs[u][:].bitcast(U32).indirect(offsets[:, s * LIST_COLS : (s + 1) * LIST_COLS])
+            nc.vector.tensor_copy(picked[:, slot[u, s], :], window)
+
+        def interleave(copy, s, n0, n1):
+            low, high = slot[0, s], slot[1, s]
+            copy(
+                grouped[s][:, PACK * n0 : PACK * n1].bitcast(F32).rearrange("p (n u) -> p n u", u=2),
+                picked[:, low : high + 1 : high - low, n0:n1].bitcast(F32).rearrange("p u n -> p n u"),
+            )
+
+        def quantize(s, n0, n1):
+            nc.vector.quantize_mx(out=codes[s][:, n0:n1].bitcast(FP8X4), scales=exps[s][:, n0:n1], in_=grouped[s][:, PACK * n0 : PACK * n1])
+
+        def layer(s, n0, n1):
+            for h in range(HALVES):
+                cols = slice(h * P, (h + 1) * P)
+                acc = psum.tile([P, n1 - n0], F32, name="acc")
+                nc.tensor.matmul_mx(
+                    out=acc[:],
+                    lhsT=w_codes[:, cols].bitcast(FP8X4),
+                    lhsT_scale=w_exps[:, cols],
+                    rhs=codes[s][:, n0:n1].bitcast(FP8X4),
+                    rhs_scale=exps[s][:, n0:n1],
+                    start=True,
+                    stop=True,
+                )
+                y = keep.tile([P, n1 - n0], F32, name="y%d_%d_%d" % (s, n0, h))
+                nc.scalar.activation(y[:], acc[:], SILU, bias=bias[:, h : h + 1])
+                nc.sync.dma_start(out[cols, s * SLICE + n0 : s * SLICE + n1], y[:])
+
+        round_shared(0, raw_low, 0, 0, HALF, 1024)
+        round_shared(0, raw_low, 0, HALF, T, HALF + 1376)
+        for s in range(SLICES):
+            gather(0, s)
+        round_pairs(nc.scalar.copy, 1, raw_high[0], 0, 0, 1536)
+        round_pairs(nc.vector.tensor_copy, 1, raw_high[0], 0, 1536, HALF)
+        round_shared(1, raw_high[1], HALF, 0, 1024, 704)
+        round_shared(1, raw_high[1], HALF, 1024, 1536, 1024 + 352)
+        round_shared(1, raw_high[1], HALF, 1536, HALF, 1536 + 352)
+
+        last = SLICES - 1
+        for s in range(last):
+            gather(1, s)
+            interleave(nc.scalar.copy, s, 0, SLICE)
+        quantize(0, 0, SLICE)
+        quantize(1, 0, SLICE)
+        gather(1, last)
+        quantize(2, 0, SLICE)
+        ends = ((0, SLICE // 2), (SLICE // 2, SLICE))
+        for n0, n1 in ends:
+            interleave(nc.vector.tensor_copy, last, n0, n1)
+        for n0, n1 in ends:
+            quantize(last, n0, n1)
+        for s in range(last):
+            layer(s, 0, SLICE)
+        for n0, n1 in ends:
+            layer(last, n0, n1)

@@ -21,6 +21,7 @@ SLICE = 512
 SLICES = S // SLICE
 LIST_COLS = SLICE // 16
 HALVES = N // P
+LAST_CHUNKS = ((0, 496, 768), (768, 1144, 1344), (1344, 1616, 1760), (1760, 1952, 2048))
 
 
 def tile_picked_pick_lin_silu_sub_e_kernel(tc, xT, w_words, w_scales, b, offs, out):
@@ -59,7 +60,7 @@ def tile_picked_pick_lin_silu_sub_e_kernel(tc, xT, w_words, w_scales, b, offs, o
         nc.sync.dma_start(offsets[:], offs)
         nc.sync.dma_start(raw_high[0][:], planes[:, 2:4, :HALF])
         nc.sync.dma_start(raw_high[1][:, 0, :], planes[:, 2, HALF:])
-        for c0, c1 in ((0, 1024), (1024, 1536), (1536, 2048)):
+        for c0, split, c1 in LAST_CHUNKS:
             nc.sync.dma_start(raw_high[1][:, 1, c0:c1], planes[:, 3, HALF + c0 : HALF + c1])
         nc.sync.dma_start(w_codes[:].bitcast(I32), w_words[0].rearrange("p n t -> p (n t)").bitcast(I32))
         with nc.allow_non_contiguous_dma(reason="one bias value to a partition"):
@@ -108,17 +109,16 @@ def tile_picked_pick_lin_silu_sub_e_kernel(tc, xT, w_words, w_scales, b, offs, o
                 )
                 y = keep.tile([P, n1 - n0], F32, name="y%d_%d_%d" % (s, n0, h))
                 nc.scalar.activation(y[:], acc[:], SILU, bias=bias[:, h : h + 1])
-                nc.sync.dma_start(out[cols, s * SLICE + n0 : s * SLICE + n1], y[:])
+                queue = nc.scalar if (s, n1, h) == (SLICES - 1, SLICE, HALVES - 1) else nc.sync
+                queue.dma_start(out[cols, s * SLICE + n0 : s * SLICE + n1], y[:])
 
         round_shared(0, raw_low, 0, 0, HALF, 1024)
         round_shared(0, raw_low, 0, HALF, T, HALF + 1376)
         for s in range(SLICES):
             gather(0, s)
-        round_pairs(nc.scalar.copy, 1, raw_high[0], 0, 0, 1536)
-        round_pairs(nc.vector.tensor_copy, 1, raw_high[0], 0, 1536, HALF)
-        round_shared(1, raw_high[1], HALF, 0, 1024, 704)
-        round_shared(1, raw_high[1], HALF, 1024, 1536, 1024 + 352)
-        round_shared(1, raw_high[1], HALF, 1536, HALF, 1536 + 352)
+        round_shared(1, raw_high[0], 0, 0, HALF, 896)
+        for c0, split, c1 in LAST_CHUNKS:
+            round_shared(1, raw_high[1], HALF, c0, c1, split)
 
         last = SLICES - 1
         for s in range(last):

@@ -94,23 +94,25 @@ def tile_picked_pick_lin_silu_sub_e_kernel(tc, xT, w_words, w_scales, b, offs, o
         def quantize(s, n0, n1):
             nc.vector.quantize_mx(out=codes[s][:, n0:n1].bitcast(FP8X4), scales=exps[s][:, n0:n1], in_=grouped[s][:, PACK * n0 : PACK * n1])
 
-        def layer(s, n0, n1):
+        def layer(s, runs):
+            accs = [psum.tile([P, SLICE], F32, name="acc") for h in range(HALVES)]
+            for n0, n1 in runs:
+                for h in range(HALVES):
+                    cols = slice(h * P, (h + 1) * P)
+                    nc.tensor.matmul_mx(
+                        out=accs[h][:, n0:n1],
+                        lhsT=w_codes[:, cols].bitcast(FP8X4),
+                        lhsT_scale=w_exps[:, cols],
+                        rhs=codes[s][:, n0:n1].bitcast(FP8X4),
+                        rhs_scale=exps[s][:, n0:n1],
+                        start=True,
+                        stop=True,
+                    )
             for h in range(HALVES):
-                cols = slice(h * P, (h + 1) * P)
-                acc = psum.tile([P, n1 - n0], F32, name="acc")
-                nc.tensor.matmul_mx(
-                    out=acc[:],
-                    lhsT=w_codes[:, cols].bitcast(FP8X4),
-                    lhsT_scale=w_exps[:, cols],
-                    rhs=codes[s][:, n0:n1].bitcast(FP8X4),
-                    rhs_scale=exps[s][:, n0:n1],
-                    start=True,
-                    stop=True,
-                )
-                y = keep.tile([P, n1 - n0], F32, name="y%d_%d_%d" % (s, n0, h))
-                nc.scalar.activation(y[:], acc[:], SILU, bias=bias[:, h : h + 1])
-                queue = nc.scalar if (s, n1, h) == (SLICES - 1, SLICE, HALVES - 1) else nc.sync
-                queue.dma_start(out[cols, s * SLICE + n0 : s * SLICE + n1], y[:])
+                y = keep.tile([P, SLICE], F32, name="y%d_%d" % (s, h))
+                nc.scalar.activation(y[:], accs[h][:], SILU, bias=bias[:, h : h + 1])
+                queue = nc.scalar if (s, h) == (SLICES - 1, HALVES - 1) else nc.sync
+                queue.dma_start(out[h * P : (h + 1) * P, s * SLICE : (s + 1) * SLICE], y[:])
 
         round_shared(0, raw_low, 0, 0, HALF, 1024)
         round_shared(0, raw_low, 0, HALF, T, HALF + 1376)
@@ -134,6 +136,5 @@ def tile_picked_pick_lin_silu_sub_e_kernel(tc, xT, w_words, w_scales, b, offs, o
         for n0, n1 in ends:
             quantize(last, n0, n1)
         for s in range(last):
-            layer(s, 0, SLICE)
-        for n0, n1 in ends:
-            layer(last, n0, n1)
+            layer(s, ((0, SLICE),))
+        layer(last, ends)

from contextlib import ExitStack

import concourse.mybir as mybir

K, T, S, N = 512, 4096, 2048, 256
FLOPS = 2 * K * S * N

F32 = mybir.dt.float32
BF16 = mybir.dt.bfloat16
I32 = mybir.dt.int32
U32 = mybir.dt.uint32
U16 = mybir.dt.uint16
U8 = mybir.dt.uint8
FP8X4 = mybir.dt.float8_e4m3fn_x4
SILU = mybir.ActivationFunctionType.Silu

P = 128
PACK = 4
HALF = T // 2
SLICE = 512
SLICES = S // SLICE
LIST_COLS = SLICE // 16
HALVES = N // P
LAST_CHUNKS = ((0, 496, 768), (768, 1144, 1344), (1344, 1616, 1760), (1760, 1952, 2048))


def tile_picked_pick_lin_silu_sub_e_kernel(tc, xT, w_words, w_scales, b, offs, out):
    nc = tc.nc
    with ExitStack() as ctx:
        keep = ctx.enter_context(tc.tile_pool(name="keep", bufs=1))
        psum = ctx.enter_context(tc.psum_pool(name="psum", bufs=8))

        offsets = keep.tile([P, S // 16], U16, name="offsets")
        w_codes = keep.tile([P, N], U32, name="w_codes", align_bytes=64)
        w_exps = keep.tile([P, N], U8, name="w_exps", align_bytes=64)
        bias = keep.tile([P, HALVES], F32, name="bias")
        warm = keep.tile([P, 8], F32, name="warm")
        warm_out = keep.tile([P, 8], F32, name="warm_out")
        raw_low = keep.tile([P, 2, T], F32, name="raw_low")
        raw_high = [keep.tile([P, 2, HALF], F32, name="raw_high%d" % i) for i in range(2)]
        pairs = [keep.tile([P, 2 * T], BF16, name="pairs%d" % u, align_bytes=64) for u in range(2)]
        picked = keep.tile([P, 2 * SLICES - 1, SLICE], U32, name="picked", align_bytes=64)
        grouped = [keep.tile([P, PACK * SLICE], BF16, name="grouped%d" % s, align_bytes=64)[:] for s in range(SLICES - 1)]
        grouped.append(picked[:, 5:7, :].rearrange("p u n -> p (u n)").bitcast(BF16))
        codes = [keep.tile([P, SLICE], U32, name="codes%d" % s, align_bytes=64) for s in range(SLICES)]
        exps = [keep.tile([P, SLICE], U8, name="exps%d" % s, align_bytes=64) for s in range(SLICES)]

        planes = xT.rearrange("(p j) t -> p j t", j=PACK)

        nc.vector.memset(w_exps[:].bitcast(I32), 0)
        nc.vector.memset(warm[:], 0.0)
        nc.scalar.activation(warm_out[:], warm[:], SILU)

        def load_scales(q):
            nc.sync.dma_start(w_exps[32 * q : 32 * q + 4, :].bitcast(I32), w_scales[0, 4 * q : 4 * q + 4, :].bitcast(I32))

        nc.sync.dma_start(raw_low[:, 0, :], planes[:, 0, :])
        nc.sync.dma_start(raw_low[:, 1, :HALF], planes[:, 1, :HALF])
        nc.sync.dma_start(raw_low[:, 1, HALF:], planes[:, 1, HALF:])
        nc.sync.dma_start(offsets[:], offs)
        nc.sync.dma_start(raw_high[0][:], planes[:, 2:4, :HALF])
        nc.sync.dma_start(raw_high[1][:, 0, :], planes[:, 2, HALF:])
        for c0, split, c1 in LAST_CHUNKS:
            nc.sync.dma_start(raw_high[1][:, 1, c0:c1], planes[:, 3, HALF + c0 : HALF + c1])
        nc.sync.dma_start(w_codes[:].bitcast(I32), w_words[0].rearrange("p n t -> p (n t)").bitcast(I32))
        with nc.allow_non_contiguous_dma(reason="one bias value to a partition"):
            nc.sync.dma_start(bias[:], b.rearrange("(h p) o -> p (h o)", p=P))
        for q in range(4):
            load_scales(q)

        def round_pairs(copy, u, raw, base, c0, c1):
            copy(
                pairs[u][:, 2 * (base + c0) : 2 * (base + c1)].rearrange("p (c e) -> p c e", e=2),
                raw[:, :, c0:c1].rearrange("p e c -> p c e"),
            )

        def round_shared(u, raw, base, c0, c1, split):
            round_pairs(nc.vector.tensor_copy, u, raw, base, c0, split)
            round_pairs(nc.scalar.copy, u, raw, base, split, c1)

        slot = {(0, 0): 1, (1, 0): 2, (0, 1): 3, (1, 1): 4, (0, 2): 5, (1, 2): 6, (0, 3): 0, (1, 3): 4}

        def gather(u, s):
            window = pairs[u][:].bitcast(U32).indirect(offsets[:, s * LIST_COLS : (s + 1) * LIST_COLS])
            nc.vector.tensor_copy(picked[:, slot[u, s], :], window)

        def interleave(copy, s, n0, n1):
            low, high = slot[0, s], slot[1, s]
            copy(
                grouped[s][:, PACK * n0 : PACK * n1].bitcast(F32).rearrange("p (n u) -> p n u", u=2),
                picked[:, low : high + 1 : high - low, n0:n1].bitcast(F32).rearrange("p u n -> p n u"),
            )

        def quantize(s, n0, n1):
            nc.vector.quantize_mx(out=codes[s][:, n0:n1].bitcast(FP8X4), scales=exps[s][:, n0:n1], in_=grouped[s][:, PACK * n0 : PACK * n1])

        def layer(s, runs):
            accs = [psum.tile([P, SLICE], F32, name="acc") for h in range(HALVES)]
            for n0, n1 in runs:
                for h in range(HALVES):
                    cols = slice(h * P, (h + 1) * P)
                    nc.tensor.matmul_mx(
                        out=accs[h][:, n0:n1],
                        lhsT=w_codes[:, cols].bitcast(FP8X4),
                        lhsT_scale=w_exps[:, cols],
                        rhs=codes[s][:, n0:n1].bitcast(FP8X4),
                        rhs_scale=exps[s][:, n0:n1],
                        start=True,
                        stop=True,
                    )
            for h in range(HALVES):
                y = keep.tile([P, SLICE], F32, name="y%d_%d" % (s, h))
                nc.scalar.activation(y[:], accs[h][:], SILU, bias=bias[:, h : h + 1])
                queue = nc.scalar if (s, h) == (SLICES - 1, HALVES - 1) else nc.sync
                queue.dma_start(out[h * P : (h + 1) * P, s * SLICE : (s + 1) * SLICE], y[:])

        round_shared(0, raw_low, 0, 0, HALF, 1024)
        round_shared(0, raw_low, 0, HALF, T, HALF + 1376)
        for s in range(SLICES):
            gather(0, s)
        round_shared(1, raw_high[0], 0, 0, HALF, 896)
        for c0, split, c1 in LAST_CHUNKS:
            round_shared(1, raw_high[1], HALF, c0, c1, split)

        last = SLICES - 1
        for s in range(last):
            gather(1, s)
            interleave(nc.scalar.copy, s, 0, SLICE)
        quantize(0, 0, SLICE)
        quantize(1, 0, SLICE)
        gather(1, last)
        quantize(2, 0, SLICE)
        ends = ((0, SLICE // 2), (SLICE // 2, SLICE))
        for n0, n1 in ends:
            interleave(nc.vector.tensor_copy, last, n0, n1)
        for n0, n1 in ends:
            quantize(last, n0, n1)
        for s in range(last):
            layer(s, ((0, SLICE),))
        layer(last, ends)
